import numpy as np
import ml_dtypes


def mxq(x, axis, fmt="e4m3"):
    dtype, down = {"e4m3": (ml_dtypes.float8_e4m3fn, 7), "e5m2": (ml_dtypes.float8_e5m2, 14)}[fmt]
    v = np.moveaxis(np.asarray(x, np.float32).astype(ml_dtypes.bfloat16).astype(np.float64), axis, -1)
    blocks = v.reshape(v.shape[:-1] + (-1, 32))
    amax = np.abs(blocks).max(-1, keepdims=True)
    byte = np.maximum(np.where(amax > 0, np.frexp(amax)[1] - 1 + 127, 0) - down, 1)
    scale = np.exp2(byte - 127.0)
    codes = (blocks / scale).astype(np.float32).astype(dtype).astype(np.float64)
    return np.moveaxis((codes * scale).reshape(v.shape), -1, axis)


WIDE = False


def mx_kscale(k):
    if not WIDE:
        return np.ones(k)
    levels = np.array([10, -10, 5, -5, 0])
    if k % 512:
        return np.exp2(np.random.permutation(np.resize(levels, k // 32))).repeat(32)
    a = np.empty((k // 512, 16))
    for p in range(k // 512):
        a[p, :8] = np.random.permutation(np.resize(levels, 8))
        for g in range(8):
            far = levels[np.abs(levels - a[p, g]) >= 10]
            a[p, g + 8] = far[np.random.randint(len(far))]
    return np.exp2(a.ravel()).repeat(32)


def f64(x):
    return np.asarray(x).astype(np.float64)


def striped(idx):
    return np.tile(np.asarray(idx).reshape(-1, 16).T, (8, 1)).astype(np.uint16)


def unstriped(offs):
    return offs[:16].T.reshape(-1).astype(np.int64)


def striped8(idx):
    return np.asarray(idx).reshape(8, -1, 16).transpose(0, 2, 1).reshape(128, -1).astype(np.uint16)


def unstriped8(offs):
    return offs.reshape(8, 16, -1).transpose(0, 2, 1).reshape(8, -1).astype(np.int64)


def pick8(x, idx, run):
    r = np.arange(len(x))
    return x[r[:, None], idx[r % (8 * run) // run]]


E2M1 = np.array([0.0, 0.5, 1.0, 1.5, 2.0, 3.0, 4.0, 6.0, -0.0, -0.5, -1.0, -1.5, -2.0, -3.0, -4.0, -6.0])


def pack_weight(w, fmt):
    k, n = w.shape
    w = f64(np.asarray(w, np.float32).astype(ml_dtypes.bfloat16)).reshape(k // 32, 32, n)
    amax = np.abs(w).max(1)
    if fmt == "e4m3":
        byte = np.frexp(amax)[1] - 1 + 127 - 7
    else:
        mant, ex = np.frexp(amax / 6.0)
        byte = np.where(mant > 0.5, ex, ex - 1) + 127
    byte = np.clip(np.where(amax > 0, byte, 1), 1, 254)
    scaled = (w * np.exp2(127.0 - byte)[:, None, :]).reshape(k, n).astype(np.float32)
    by_word = np.ascontiguousarray(scaled.reshape(k // 512, 128, 4, n).transpose(0, 1, 3, 2))
    if fmt == "e4m3":
        words = by_word.astype(ml_dtypes.float8_e4m3fn).view(np.uint8)
    else:
        c = by_word.astype(ml_dtypes.float4_e2m1fn).view(np.uint8) & 0xF
        words = (c[..., 0::2] | (c[..., 1::2] << 4)).reshape(k // 512, 128, 2 * n)
    return np.ascontiguousarray(words), np.ascontiguousarray(byte.astype(np.uint8).reshape(k // 512, 16, n))


def unpack_weight(words, scales, fmt):
    g, _, n = scales.shape
    words = np.ascontiguousarray(words).reshape(g, 128, n, -1)
    if fmt == "e4m3":
        vals = words.view(ml_dtypes.float8_e4m3fn).astype(np.float64)
    else:
        nib = np.empty((g, 128, n, 4), np.uint8)
        nib[..., 0::2] = words & 0xF
        nib[..., 1::2] = words >> 4
        vals = E2M1[nib]
    vals = vals * np.repeat(np.exp2(scales.astype(np.float64) - 127.0), 8, axis=1)[..., None]
    return vals.transpose(0, 1, 3, 2).reshape(g * 512, n)


K, J, R, T, Z, M, C, S, N, V = 512, 512, 512, 1024, 512, 1024, 1024, 256, 256, 1024


def setup_inputs():
    n = np.random.standard_normal
    idx = np.random.permutation(T)[:J]
    idx2 = np.random.permutation(M)[:J]
    idx3 = np.stack([np.random.permutation(C)[:J] for _ in range(8)])
    idx4 = np.stack([np.random.permutation(C)[:S] for _ in range(8)])
    idx5 = np.stack([np.random.permutation(J)[:S] for _ in range(8)])
    idx6 = np.random.permutation(V)[:N]
    fk = mx_kscale(K)
    fr = mx_kscale(R)
    fz = mx_kscale(Z)
    xtp = pack_weight(n((K, T)) * fk[:, None], "e2m1")
    wp = pack_weight(n((K, R)) * 1 / np.sqrt(K) / fk[:, None] * fr, "e4m3")
    xop = pack_weight(n((Z, M)) / fz[:, None], "e4m3")
    w2p = pack_weight(n((Z, R)) * 1 / np.sqrt(Z) * fz[:, None] * fr, "e2m1")
    vsp = pack_weight(n((R, V)) * 1 / np.sqrt(R) / fr[:, None], "e2m1")
    return {
        "xt_words": xtp[0],
        "xt_scales": xtp[1],
        "w_words": wp[0],
        "w_scales": wp[1],
        "xo_words": xop[0],
        "xo_scales": xop[1],
        "w2_words": w2p[0],
        "w2_scales": w2p[1],
        "sa": (np.random.uniform(0.5, 1.6, (R, 1))).astype(np.float32),
        "vs_words": vsp[0],
        "vs_scales": vsp[1],
        "offs": striped(idx),
        "offs2": striped(idx2),
        "offs3": striped8(idx3),
        "offs4": striped8(idx4),
        "offs5": striped8(idx5),
        "offs6": striped(idx6),
    }


def reference(xt_words, xt_scales, w_words, w_scales, xo_words, xo_scales, w2_words, w2_scales, sa, vs_words, vs_scales, offs, offs2, offs3, offs4, offs5, offs6):
    idx = unstriped(offs)
    idx2 = unstriped(offs2)
    idx3 = unstriped8(offs3)
    idx4 = unstriped8(offs4)
    idx5 = unstriped8(offs5)
    idx6 = unstriped(offs6)
    xtu = unpack_weight(xt_words, xt_scales, "e2m1")
    wu = unpack_weight(w_words, w_scales, "e4m3")
    xou = unpack_weight(xo_words, xo_scales, "e4m3")
    w2u = unpack_weight(w2_words, w2_scales, "e2m1")
    vsu = unpack_weight(vs_words, vs_scales, "e2m1")
    xtidxg = xtu[:, idx]
    a = wu.T @ xtidxg
    xoidx2g = xou[:, idx2]
    b = w2u.T @ xoidx2g
    pw = np.zeros((R, C))
    pw[np.arange(R)[:, None], idx3[np.arange(R) % 512 // 64]] = a
    h1 = pick8(pw, idx4, 64) * f64(sa)
    pv = np.zeros((R, J))
    pv[np.arange(R)[:, None], idx5[np.arange(R) % 512 // 64]] = h1
    hid = np.maximum(b, pv)
    vsidx6g = vsu[:, idx6]
    hidq = mxq(hid, 0, "e4m3")
    y = vsidx6g.T @ hidq
    return y

@@ -1,0 +1,276 @@
+from contextlib import ExitStack
+
+import concourse.mybir as mybir
+
+F32 = mybir.dt.float32
+BF16 = mybir.dt.bfloat16
+I32 = mybir.dt.int32
+U32 = mybir.dt.uint32
+U16 = mybir.dt.uint16
+U8 = mybir.dt.uint8
+FP8X4 = mybir.dt.float8_e4m3fn_x4
+FP4X4 = mybir.dt.float4_e2m1fn_x4
+COPY = mybir.ActivationFunctionType.Copy
+MAX = mybir.AluOpType.max
+
+P = 128
+PACK = 4
+J, R, T, M, C, S, N, V = 512, 512, 1024, 1024, 1024, 256, 256, 1024
+FIRST = 128
+HALF = J // 2
+FLOPS = 2 * 512 * R * J * 2 + 2 * R * N * J
+
+
+def tile_picked_tokens_plain_two_returned_store_plain_kernel(
+    tc, xt_words, xt_scales, w_words, w_scales, xo_words, xo_scales, w2_words, w2_scales,
+    sa, vs_words, vs_scales, offs, offs2, offs3, offs4, offs5, offs6, out,
+):
+    nc = tc.nc
+    with ExitStack() as ctx:
+        keep = ctx.enter_context(tc.tile_pool(name="keep", bufs=1))
+        psum = ctx.enter_context(tc.psum_pool(name="psum", bufs=8))
+
+        def sb(name, shape, dtype, tag=None):
+            return keep.tile(shape, dtype, name=name, tag=tag or name, align_bytes=64)
+
+        def bank(name, width):
+            return psum.tile([P, width], F32, name=name, tag="bank")
+
+        def load_list(name, src):
+            tile = sb(name, list(src.shape), U16)
+            nc.sync.dma_start(tile[:], src)
+            return tile
+
+        def load_scale_rows(tile, src):
+            for q in range(4):
+                nc.sync.dma_start(tile[32 * q : 32 * q + 4, :].bitcast(I32), src[0, 4 * q : 4 * q + 4, :].bitcast(I32))
+
+        def zero_bytes(tile):
+            nc.vector.memset(tile[:].bitcast(I32), 0)
+
+        def entries(lst, lo, hi):
+            return lst[:, lo // 16 : hi // 16]
+
+        xt_s = sb("xt_s", [P, T], U8, tag="shared")
+        zero_bytes(xt_s)
+        w_rows = sb("w_rows", [P, R], U8)
+        zero_bytes(w_rows)
+
+        def stage_scale_rows(name, src):
+            tile = sb(name, [4, 4, src.shape[2] // 4], I32)
+            nc.sync.dma_start(tile[:], src[0].bitcast(I32).rearrange("(q r) c -> r q c", r=4))
+            return tile
+
+        def spread_scale_rows(tile, stage):
+            for q in (1, 2, 3, 0):
+                nc.vector.tensor_copy(tile[32 * q : 32 * q + 4, :].bitcast(I32), stage[:, q, :])
+
+        w_stage = stage_scale_rows("w_stage", w_scales)
+        lst1 = load_list("lst1", offs)
+        xt_w = sb("xt_w", [P, T], U16)
+        nc.sync.dma_start(xt_w[:].bitcast(I32), xt_words[0].bitcast(I32))
+        load_scale_rows(xt_s, xt_scales)
+        w_raw = sb("w_raw", [P, R], U32)
+        nc.scalar.dma_start(w_raw[:].bitcast(I32), w_words[0].rearrange("p c k -> p (c k)").bitcast(I32))
+        lst3 = load_list("lst3", offs3)
+
+        boards = [sb("board%d" % i, [P, C], F32) for i in range(2)]
+        nc.vector.memset(boards[0][:], 0.0)
+
+        nc.gpsimd.memset(boards[1][:], 0.0)
+        spread_scale_rows(w_rows, w_stage)
+        ws_by_tile = w_rows[:].rearrange("p (m t) -> p t m", t=PACK)
+        ws_lo = sb("ws_lo", [P, 2, P], U8)
+        nc.vector.tensor_copy(ws_lo[:], ws_by_tile[:, 0:2, :])
+        ws_hi = sb("ws_hi", [P, 2, P], U8)
+        ws_tiles = [ws_lo[:, 0, :], ws_lo[:, 1, :], ws_hi[:, 0, :], ws_hi[:, 1, :]]
+
+        w_by_column = w_raw[:].rearrange("p (m t) -> p m t", t=PACK)
+        w_lo = sb("w_lo", [P, 2, P], U32)
+        nc.scalar.copy(w_lo[:].rearrange("p t m -> p m t"), w_by_column[:, :, 0:2])
+
+        pieces = ((0, 128), (128, 256), (256, J))
+        xt_gw = [sb("xt_gw0", [P, 128], U16)]
+        nc.vector.tensor_copy(xt_gw[0][:], xt_w[:].indirect(entries(lst1, 0, 128)))
+        xt_gs = []
+        for i, (lo, hi) in enumerate(pieces):
+            xt_gs.append(sb("xt_gs%d" % i, [P, hi - lo], U8))
+            nc.vector.tensor_copy(xt_gs[i][:], xt_s[:].indirect(entries(lst1, lo, hi)))
+        later = sb("xt_gw_later", [P, J - 128], U16, tag="shared")
+        for lo, hi in pieces[1:]:
+            nc.vector.tensor_copy(later[:, lo - 128 : hi - 128], xt_w[:].indirect(entries(lst1, lo, hi)))
+        xt_words_of = [xt_gw[0][:], later[:, 0:128], later[:, 128:]]
+
+        w_hi = sb("w_hi", [P, 2, P], U32)
+        w_tiles = [w_lo[:, 0, :], w_lo[:, 1, :], w_hi[:, 0, :], w_hi[:, 1, :]]
+
+        def product_a(dst, t, i):
+            nc.tensor.matmul_mx(
+                dst, lhsT=w_tiles[t].bitcast(FP8X4), lhsT_scale=ws_tiles[t],
+                rhs=xt_words_of[i].bitcast(FP4X4), rhs_scale=xt_gs[i][:], start=True, stop=True,
+            )
+
+        def scatter(window, offsets, values):
+            nc.scalar.activation(window[:].indirect(offsets), values, COPY)
+
+        a_first = []
+        for t in range(2):
+            ps = bank("first_ps%d" % t, 128)
+            product_a(ps[:], t, 0)
+            a_first.append(sb("a_first%d" % t, [P, 128], F32))
+            nc.scalar.copy(a_first[t][:], ps[:])
+        for t in range(2):
+            scatter(boards[t], entries(lst3, 0, 128), a_first[t][:])
+
+        a_later = {}
+        for i in (1, 2):
+            width = pieces[i][1] - pieces[i][0]
+            ps = bank("later_ps%d" % i, 2 * width)
+            for t in range(2):
+                product_a(ps[:, t * width : (t + 1) * width], t, i)
+            a_later[i] = sb("a_later%d" % i, [P, 2, width], F32)
+            nc.vector.tensor_copy(a_later[i][:].rearrange("p t j -> p (t j)"), ps[:])
+
+        nc.gpsimd.tensor_copy(
+            w_hi[:].bitcast(I32).rearrange("p t m -> p m t"),
+            w_raw[:].bitcast(I32).rearrange("p (m t) -> p m t", t=PACK)[:, :, 2:4],
+        )
+        nc.gpsimd.tensor_copy(ws_hi[:], ws_by_tile[:, 2:4, :])
+        a_whole = {}
+        for t in range(2, PACK):
+            ps = bank("a_ps%d" % t, J)
+            for i, (lo, hi) in enumerate(pieces):
+                product_a(ps[:, lo:hi], t, i)
+            a_whole[t] = sb("a_whole%d" % t, [P, J], F32)
+            nc.vector.tensor_copy(a_whole[t][:], ps[:])
+
+        lst4 = load_list("lst4", offs4)
+        sa_sb = sb("sa_sb", [P, PACK], F32)
+        nc.sync.dma_start(sa_sb[:], sa.rearrange("(p t) o -> p (t o)", t=PACK))
+        lst5 = load_list("lst5", offs5)
+        lst2 = load_list("lst2", offs2)
+        xo_s = sb("xo_s", [P, M], U8)
+        zero_bytes(xo_s)
+        load_scale_rows(xo_s, xo_scales)
+        w2_rows = sb("w2_rows", [P, R], U8)
+        zero_bytes(w2_rows)
+        load_scale_rows(w2_rows, w2_scales)
+        xo_w = sb("xo_w", [P, M], U32)
+        nc.sync.dma_start(xo_w[:].bitcast(I32), xo_words[0].rearrange("p c k -> p (c k)").bitcast(I32))
+        w2_raw = sb("w2_raw", [P, 2 * R], U8)
+        nc.sync.dma_start(w2_raw[:].bitcast(I32), w2_words[0].bitcast(I32))
+        lst6 = load_list("lst6", offs6)
+        vs_s = sb("vs_s", [P, V], U8)
+        zero_bytes(vs_s)
+        load_scale_rows(vs_s, vs_scales)
+        vs_w = sb("vs_w", [P, V], U16)
+        nc.sync.dma_start(vs_w[:].bitcast(I32), vs_words[0].bitcast(I32))
+
+        slots = [sb("slots%d" % i, [P, J], F32) for i in range(2)]
+        for tile in slots:
+            nc.vector.memset(tile[:], 0.0)
+
+        w2_w = sb("w2_w", [P, PACK, P, 2], U8)
+        nc.vector.tensor_copy(w2_w[:], w2_raw[:].rearrange("p (m t b) -> p t m b", t=PACK, b=2))
+        w2_s = sb("w2_s", [P, PACK, P], U8)
+        nc.vector.tensor_copy(w2_s[:], w2_rows[:].rearrange("p (m t) -> p t m", t=PACK))
+        xo_gw = sb("xo_gw", [P, J], U32)
+        xo_gs = sb("xo_gs", [P, J], U8)
+        nc.vector.tensor_copy(xo_gw[:], xo_w[:].indirect(lst2[:]))
+        nc.vector.tensor_copy(xo_gs[:], xo_s[:].indirect(lst2[:]))
+        b_ps = []
+        for t in range(PACK):
+            ps = bank("b_ps%d" % t, J)
+            nc.tensor.matmul_mx(
+                ps[:], lhsT=w2_w[:, t, :, :].rearrange("p m b -> p (m b)").bitcast(FP4X4), lhsT_scale=w2_s[:, t, :],
+                rhs=xo_gw[:].bitcast(FP8X4), rhs_scale=xo_gs[:], start=True, stop=True,
+            )
+            b_ps.append(ps)
+
+        vs_gw = sb("vs_gw", [P, N], U16)
+        vs_gs = sb("vs_gs", [P, N], U8)
+        nc.vector.tensor_copy(vs_gw[:], vs_w[:].indirect(lst6[:]))
+        nc.vector.tensor_copy(vs_gs[:], vs_s[:].indirect(lst6[:]))
+
+        groups = ((0, 128), (128, 256), (256, J))
+        planes = [sb("planes%d" % g, [P, PACK, hi - lo], BF16) for g, (lo, hi) in enumerate(groups)]
+        hid = [sb("hid%d" % c, [P, 128, PACK], BF16) for c in range(4)]
+        returns = [sb("returns%d" % t, [P, S], F32) for t in range(PACK)]
+
+        def fetch(t):
+            nc.scalar.activation(returns[t][:], boards[t % 2][:].indirect(lst4[:]), COPY, scale=sa_sb[:, t : t + 1])
+
+        def put_back(t):
+            scatter(slots[t % 2], lst5[:], returns[t][:])
+
+        def larger(t, g):
+            lo, hi = groups[g]
+            nc.vector.tensor_tensor(planes[g][:, t, :], slots[t % 2][:, lo:hi], b_ps[t][:, lo:hi], MAX)
+
+        def weave(copy, t, c):
+            g = min(c, 2)
+            lo = 128 * c - groups[g][0]
+            copy(hid[c][:, :, t : t + 2], planes[g][:, t : t + 2, lo : lo + 128].rearrange("p t j -> p j t"))
+
+        for i in (1, 2):
+            for t in range(2):
+                scatter(boards[t], entries(lst3, pieces[i][0], pieces[i][1]), a_later[i][:, t, :])
+        for t in range(2):
+            fetch(t)
+        for t in range(2):
+            scatter(boards[t], lst3[:], a_whole[t + 2][:])
+            put_back(t)
+            for g in range(3):
+                larger(t, g)
+        for c in range(4):
+            weave(nc.vector.tensor_copy, 0, c)
+        for t in range(2, PACK):
+            fetch(t)
+        put_back(2)
+        for g in range(3):
+            larger(2, g)
+        put_back(3)
+
+        codes = [sb("codes%d" % c, [P, 128], U32) for c in range(4)]
+        scales = [sb("scales%d" % c, [P, 128], U8) for c in range(4)]
+
+        def quantise(c):
+            nc.vector.quantize_mx(
+                out=codes[c][:].bitcast(FP8X4), scales=scales[c][:], in_=hid[c][:].rearrange("p j t -> p (j t)")
+            )
+
+        def product_y(dst, u, c):
+            rows = slice(u * P, (u + 1) * P)
+            nc.tensor.matmul_mx(
+                dst, lhsT=vs_gw[:, rows].bitcast(FP4X4), lhsT_scale=vs_gs[:, rows],
+                rhs=codes[c][:].bitcast(FP8X4), rhs_scale=scales[c][:], start=True, stop=True,
+            )
+
+        def finish(c, copy):
+            ps = bank("y_ps%d" % c, 256)
+            for u in range(2):
+                product_y(ps[:, u * 128 : (u + 1) * 128], u, c)
+            y = sb("y%d" % c, [P, 2, 128], F32)
+            copy(y[:].rearrange("p u j -> p (u j)"), ps[:])
+            nc.sync.dma_start(out[:, 128 * c : 128 * (c + 1)].rearrange("(u p) j -> p u j", u=2), y[:])
+
+        larger(3, 0)
+        larger(3, 2)
+        weave(nc.scalar.copy, 2, 2)
+        weave(nc.scalar.copy, 2, 3)
+        weave(nc.vector.tensor_copy, 2, 0)
+        larger(3, 1)
+        quantise(0)
+        weave(nc.vector.tensor_copy, 2, 1)
+        quantise(2)
+        quantise(1)
+        quantise(3)
+        finish(0, nc.scalar.copy)
+        finish(2, nc.scalar.copy)
+        finish(1, nc.vector.tensor_copy)
+        for u, copy, queue in ((0, nc.scalar.copy, nc.scalar), (1, nc.vector.tensor_copy, nc.sync)):
+            ps = bank("y_ps3%d" % u, 128)
+            product_y(ps[:], u, 3)
+            y = sb("y3%d" % u, [P, 128], F32)
+            copy(y[:], ps[:])
+            queue.dma_start(out[u * P : (u + 1) * P, 384:512], y[:])

@@ -28,10 +28,14 @@ def tile_picked_tokens_plain_two_returned_store_plain_kernel(
     nc = tc.nc
     with ExitStack() as ctx:
         keep = ctx.enter_context(tc.tile_pool(name="keep", bufs=1))
+        turns = ctx.enter_context(tc.tile_pool(name="turns", bufs=1))
         psum = ctx.enter_context(tc.psum_pool(name="psum", bufs=8))
 
         def sb(name, shape, dtype, tag=None):
             return keep.tile(shape, dtype, name=name, tag=tag or name, align_bytes=64)
+
+        def tenant(name, shape, dtype, offset):
+            return turns.tile(shape, dtype, name=name, align_bytes=64, offset=offset)
 
         def bank(name, width):
             return psum.tile([P, width], F32, name=name, tag="bank")
@@ -45,16 +49,16 @@ def tile_picked_tokens_plain_two_returned_store_plain_kernel(
             for q in range(4):
                 nc.sync.dma_start(tile[32 * q : 32 * q + 4, :].bitcast(I32), src[0, 4 * q : 4 * q + 4, :].bitcast(I32))
 
-        def zero_bytes(tile):
-            nc.vector.memset(tile[:].bitcast(I32), 0)
+        def zero_bytes(engine, tile):
+            engine.memset(tile[:].bitcast(I32), 0)
 
         def entries(lst, lo, hi):
             return lst[:, lo // 16 : hi // 16]
 
         xt_s = sb("xt_s", [P, T], U8, tag="shared")
-        zero_bytes(xt_s)
+        zero_bytes(nc.vector, xt_s)
         w_rows = sb("w_rows", [P, R], U8)
-        zero_bytes(w_rows)
+        zero_bytes(nc.vector, w_rows)
 
         def stage_scale_rows(name, src):
             tile = sb(name, [4, 4, src.shape[2] // 4], I32)
@@ -67,7 +71,7 @@ def tile_picked_tokens_plain_two_returned_store_plain_kernel(
 
         w_stage = stage_scale_rows("w_stage", w_scales)
         lst1 = load_list("lst1", offs)
-        xt_w = sb("xt_w", [P, T], U16)
+        xt_w = tenant("xt_w", [P, T], U16, 0)
         nc.sync.dma_start(xt_w[:].bitcast(I32), xt_words[0].bitcast(I32))
         load_scale_rows(xt_s, xt_scales)
         w_raw = sb("w_raw", [P, R], U32)
@@ -77,17 +81,16 @@ def tile_picked_tokens_plain_two_returned_store_plain_kernel(
         boards = [sb("board%d" % i, [P, C], F32) for i in range(2)]
         nc.vector.memset(boards[0][:], 0.0)
 
-        nc.gpsimd.memset(boards[1][:], 0.0)
+        nc.vector.memset(boards[1][:], 0.0)
         spread_scale_rows(w_rows, w_stage)
         ws_by_tile = w_rows[:].rearrange("p (m t) -> p t m", t=PACK)
         ws_lo = sb("ws_lo", [P, 2, P], U8)
         nc.vector.tensor_copy(ws_lo[:], ws_by_tile[:, 0:2, :])
-        ws_hi = sb("ws_hi", [P, 2, P], U8)
+        ws_hi = tenant("ws_hi", [P, 2, P], U8, 0)
         ws_tiles = [ws_lo[:, 0, :], ws_lo[:, 1, :], ws_hi[:, 0, :], ws_hi[:, 1, :]]
 
-        w_by_column = w_raw[:].rearrange("p (m t) -> p m t", t=PACK)
-        w_lo = sb("w_lo", [P, 2, P], U32)
-        nc.scalar.copy(w_lo[:].rearrange("p t m -> p m t"), w_by_column[:, :, 0:2])
+        w_w = sb("w_w", [P, PACK, P], U32)
+        nc.scalar.copy(w_w[:].rearrange("p t m -> p m t"), w_raw[:].rearrange("p (m t) -> p m t", t=PACK))
 
         pieces = ((0, 128), (128, 256), (256, J))
         xt_gw = [sb("xt_gw0", [P, 128], U16)]
@@ -101,12 +104,10 @@ def tile_picked_tokens_plain_two_returned_store_plain_kernel(
             nc.vector.tensor_copy(later[:, lo - 128 : hi - 128], xt_w[:].indirect(entries(lst1, lo, hi)))
         xt_words_of = [xt_gw[0][:], later[:, 0:128], later[:, 128:]]
 
-        w_hi = sb("w_hi", [P, 2, P], U32)
-        w_tiles = [w_lo[:, 0, :], w_lo[:, 1, :], w_hi[:, 0, :], w_hi[:, 1, :]]
 
         def product_a(dst, t, i):
             nc.tensor.matmul_mx(
-                dst, lhsT=w_tiles[t].bitcast(FP8X4), lhsT_scale=ws_tiles[t],
+                dst, lhsT=w_w[:, t, :].bitcast(FP8X4), lhsT_scale=ws_tiles[t],
                 rhs=xt_words_of[i].bitcast(FP4X4), rhs_scale=xt_gs[i][:], start=True, stop=True,
             )
 
@@ -117,7 +118,7 @@ def tile_picked_tokens_plain_two_returned_store_plain_kernel(
         for t in range(2):
             ps = bank("first_ps%d" % t, 128)
             product_a(ps[:], t, 0)
-            a_first.append(sb("a_first%d" % t, [P, 128], F32))
+            a_first.append(tenant("a_first%d" % t, [P, 128], F32, 2048 + 512 * t))
             nc.scalar.copy(a_first[t][:], ps[:])
         for t in range(2):
             scatter(boards[t], entries(lst3, 0, 128), a_first[t][:])
@@ -128,47 +129,42 @@ def tile_picked_tokens_plain_two_returned_store_plain_kernel(
             ps = bank("later_ps%d" % i, 2 * width)
             for t in range(2):
                 product_a(ps[:, t * width : (t + 1) * width], t, i)
-            a_later[i] = sb("a_later%d" % i, [P, 2, width], F32)
+            a_later[i] = tenant("a_later%d" % i, [P, 2, width], F32, 2048 + 1024 * i)
             nc.vector.tensor_copy(a_later[i][:].rearrange("p t j -> p (t j)"), ps[:])
 
-        nc.gpsimd.tensor_copy(
-            w_hi[:].bitcast(I32).rearrange("p t m -> p m t"),
-            w_raw[:].bitcast(I32).rearrange("p (m t) -> p m t", t=PACK)[:, :, 2:4],
-        )
         nc.gpsimd.tensor_copy(ws_hi[:], ws_by_tile[:, 2:4, :])
-        a_whole = {}
-        for t in range(2, PACK):
-            ps = bank("a_ps%d" % t, J)
-            for i, (lo, hi) in enumerate(pieces):
-                product_a(ps[:, lo:hi], t, i)
-            a_whole[t] = sb("a_whole%d" % t, [P, J], F32)
-            nc.vector.tensor_copy(a_whole[t][:], ps[:])
+        a_pair = sb("a_pair", [P, 2, J], F32)
+        for h in range(2):
+            ps = bank("pair_ps%d" % h, J)
+            for t in range(2, PACK):
+                for i, (lo, hi) in enumerate(pieces):
+                    if lo // HALF == h:
+                        at = (t - 2) * HALF + lo - h * HALF
+                        product_a(ps[:, at : at + hi - lo], t, i)
+            nc.vector.tensor_copy(a_pair[:, :, h * HALF : (h + 1) * HALF], ps[:].rearrange("p (t j) -> p t j", t=2))
 
         lst4 = load_list("lst4", offs4)
         sa_sb = sb("sa_sb", [P, PACK], F32)
         nc.sync.dma_start(sa_sb[:], sa.rearrange("(p t) o -> p (t o)", t=PACK))
         lst5 = load_list("lst5", offs5)
         lst2 = load_list("lst2", offs2)
-        xo_s = sb("xo_s", [P, M], U8)
-        zero_bytes(xo_s)
+        xo_s = tenant("xo_s", [P, M], U8, 1024)
+        zero_bytes(nc.gpsimd, xo_s)
         load_scale_rows(xo_s, xo_scales)
-        w2_rows = sb("w2_rows", [P, R], U8)
-        zero_bytes(w2_rows)
+        w2_rows = tenant("w2_rows", [P, R], U8, 256)
+        zero_bytes(nc.gpsimd, w2_rows)
         load_scale_rows(w2_rows, w2_scales)
         xo_w = sb("xo_w", [P, M], U32)
         nc.sync.dma_start(xo_w[:].bitcast(I32), xo_words[0].rearrange("p c k -> p (c k)").bitcast(I32))
         w2_raw = sb("w2_raw", [P, 2 * R], U8)
         nc.sync.dma_start(w2_raw[:].bitcast(I32), w2_words[0].bitcast(I32))
         lst6 = load_list("lst6", offs6)
-        vs_s = sb("vs_s", [P, V], U8)
-        zero_bytes(vs_s)
+        vs_s = sb("vs_s", [P, V], U8, tag="shared")
+        zero_bytes(nc.gpsimd, vs_s)
         load_scale_rows(vs_s, vs_scales)
         vs_w = sb("vs_w", [P, V], U16)
         nc.sync.dma_start(vs_w[:].bitcast(I32), vs_words[0].bitcast(I32))
 
-        slots = [sb("slots%d" % i, [P, J], F32) for i in range(2)]
-        for tile in slots:
-            nc.vector.memset(tile[:], 0.0)
 
         w2_w = sb("w2_w", [P, PACK, P, 2], U8)
         nc.vector.tensor_copy(w2_w[:], w2_raw[:].rearrange("p (m t b) -> p t m b", t=PACK, b=2))
@@ -215,13 +211,17 @@ def tile_picked_tokens_plain_two_returned_store_plain_kernel(
         for i in (1, 2):
             for t in range(2):
                 scatter(boards[t], entries(lst3, pieces[i][0], pieces[i][1]), a_later[i][:, t, :])
+        slots = [tenant("slots%d" % i, [P, J], F32, 2048 + 2048 * i) for i in range(2)]
+        for tile in slots:
+            nc.gpsimd.memset(tile[:], 0.0)
         for t in range(2):
             fetch(t)
         for t in range(2):
-            scatter(boards[t], lst3[:], a_whole[t + 2][:])
             put_back(t)
             for g in range(3):
                 larger(t, g)
+        for t in range(2):
+            scatter(boards[t], lst3[:], a_pair[:, t, :])
         for c in range(4):
             weave(nc.vector.tensor_copy, 0, c)
         for t in range(2, PACK):

from contextlib import ExitStack

import concourse.mybir as mybir

F32 = mybir.dt.float32
BF16 = mybir.dt.bfloat16
I32 = mybir.dt.int32
U32 = mybir.dt.uint32
U16 = mybir.dt.uint16
U8 = mybir.dt.uint8
FP8X4 = mybir.dt.float8_e4m3fn_x4
FP4X4 = mybir.dt.float4_e2m1fn_x4
COPY = mybir.ActivationFunctionType.Copy
MAX = mybir.AluOpType.max

P = 128
PACK = 4
J, R, T, M, C, S, N, V = 512, 512, 1024, 1024, 1024, 256, 256, 1024
FIRST = 128
HALF = J // 2
FLOPS = 2 * 512 * R * J * 2 + 2 * R * N * J


def tile_picked_tokens_plain_two_returned_store_plain_kernel(
    tc, xt_words, xt_scales, w_words, w_scales, xo_words, xo_scales, w2_words, w2_scales,
    sa, vs_words, vs_scales, offs, offs2, offs3, offs4, offs5, offs6, out,
):
    nc = tc.nc
    with ExitStack() as ctx:
        keep = ctx.enter_context(tc.tile_pool(name="keep", bufs=1))
        turns = ctx.enter_context(tc.tile_pool(name="turns", bufs=1))
        psum = ctx.enter_context(tc.psum_pool(name="psum", bufs=8))

        def sb(name, shape, dtype, tag=None):
            return keep.tile(shape, dtype, name=name, tag=tag or name, align_bytes=64)

        def tenant(name, shape, dtype, offset):
            return turns.tile(shape, dtype, name=name, align_bytes=64, offset=offset)

        def bank(name, width):
            return psum.tile([P, width], F32, name=name, tag="bank")

        def load_list(name, src):
            tile = sb(name, list(src.shape), U16)
            nc.sync.dma_start(tile[:], src)
            return tile

        def load_scale_rows(tile, src):
            for q in range(4):
                nc.sync.dma_start(tile[32 * q : 32 * q + 4, :].bitcast(I32), src[0, 4 * q : 4 * q + 4, :].bitcast(I32))

        def zero_bytes(engine, tile):
            engine.memset(tile[:].bitcast(I32), 0)

        def entries(lst, lo, hi):
            return lst[:, lo // 16 : hi // 16]

        xt_s = sb("xt_s", [P, T], U8, tag="shared")
        zero_bytes(nc.vector, xt_s)
        w_rows = sb("w_rows", [P, R], U8)
        zero_bytes(nc.vector, w_rows)

        def stage_scale_rows(name, src):
            tile = sb(name, [4, 4, src.shape[2] // 4], I32)
            nc.sync.dma_start(tile[:], src[0].bitcast(I32).rearrange("(q r) c -> r q c", r=4))
            return tile

        def spread_scale_rows(tile, stage):
            for q in (1, 2, 3, 0):
                nc.vector.tensor_copy(tile[32 * q : 32 * q + 4, :].bitcast(I32), stage[:, q, :])

        w_stage = stage_scale_rows("w_stage", w_scales)
        lst1 = load_list("lst1", offs)
        xt_w = tenant("xt_w", [P, T], U16, 0)
        nc.sync.dma_start(xt_w[:].bitcast(I32), xt_words[0].bitcast(I32))
        load_scale_rows(xt_s, xt_scales)
        w_raw = sb("w_raw", [P, R], U32)
        nc.scalar.dma_start(w_raw[:].bitcast(I32), w_words[0].rearrange("p c k -> p (c k)").bitcast(I32))
        lst3 = load_list("lst3", offs3)

        boards = [sb("board%d" % i, [P, C], F32) for i in range(2)]
        nc.vector.memset(boards[0][:], 0.0)

        nc.vector.memset(boards[1][:], 0.0)
        spread_scale_rows(w_rows, w_stage)
        ws_by_tile = w_rows[:].rearrange("p (m t) -> p t m", t=PACK)
        ws_lo = sb("ws_lo", [P, 2, P], U8)
        nc.vector.tensor_copy(ws_lo[:], ws_by_tile[:, 0:2, :])
        ws_hi = tenant("ws_hi", [P, 2, P], U8, 0)
        ws_tiles = [ws_lo[:, 0, :], ws_lo[:, 1, :], ws_hi[:, 0, :], ws_hi[:, 1, :]]

        w_w = sb("w_w", [P, PACK, P], U32)
        nc.scalar.copy(w_w[:].rearrange("p t m -> p m t"), w_raw[:].rearrange("p (m t) -> p m t", t=PACK))

        pieces = ((0, 128), (128, 256), (256, J))
        xt_gw = [sb("xt_gw0", [P, 128], U16)]
        nc.vector.tensor_copy(xt_gw[0][:], xt_w[:].indirect(entries(lst1, 0, 128)))
        xt_gs = []
        for i, (lo, hi) in enumerate(pieces):
            xt_gs.append(sb("xt_gs%d" % i, [P, hi - lo], U8))
            nc.vector.tensor_copy(xt_gs[i][:], xt_s[:].indirect(entries(lst1, lo, hi)))
        later = sb("xt_gw_later", [P, J - 128], U16, tag="shared")
        for lo, hi in pieces[1:]:
            nc.vector.tensor_copy(later[:, lo - 128 : hi - 128], xt_w[:].indirect(entries(lst1, lo, hi)))
        xt_words_of = [xt_gw[0][:], later[:, 0:128], later[:, 128:]]


        def product_a(dst, t, i):
            nc.tensor.matmul_mx(
                dst, lhsT=w_w[:, t, :].bitcast(FP8X4), lhsT_scale=ws_tiles[t],
                rhs=xt_words_of[i].bitcast(FP4X4), rhs_scale=xt_gs[i][:], start=True, stop=True,
            )

        def scatter(window, offsets, values):
            nc.scalar.activation(window[:].indirect(offsets), values, COPY)

        a_first = []
        for t in range(2):
            ps = bank("first_ps%d" % t, 128)
            product_a(ps[:], t, 0)
            a_first.append(tenant("a_first%d" % t, [P, 128], F32, 2048 + 512 * t))
            nc.scalar.copy(a_first[t][:], ps[:])
        for t in range(2):
            scatter(boards[t], entries(lst3, 0, 128), a_first[t][:])

        a_later = {}
        for i in (1, 2):
            width = pieces[i][1] - pieces[i][0]
            ps = bank("later_ps%d" % i, 2 * width)
            for t in range(2):
                product_a(ps[:, t * width : (t + 1) * width], t, i)
            a_later[i] = tenant("a_later%d" % i, [P, 2, width], F32, 2048 + 1024 * i)
            nc.vector.tensor_copy(a_later[i][:].rearrange("p t j -> p (t j)"), ps[:])

        nc.gpsimd.tensor_copy(ws_hi[:], ws_by_tile[:, 2:4, :])
        a_pair = sb("a_pair", [P, 2, J], F32)
        for h in range(2):
            ps = bank("pair_ps%d" % h, J)
            for t in range(2, PACK):
                for i, (lo, hi) in enumerate(pieces):
                    if lo // HALF == h:
                        at = (t - 2) * HALF + lo - h * HALF
                        product_a(ps[:, at : at + hi - lo], t, i)
            nc.vector.tensor_copy(a_pair[:, :, h * HALF : (h + 1) * HALF], ps[:].rearrange("p (t j) -> p t j", t=2))

        lst4 = load_list("lst4", offs4)
        sa_sb = sb("sa_sb", [P, PACK], F32)
        nc.sync.dma_start(sa_sb[:], sa.rearrange("(p t) o -> p (t o)", t=PACK))
        lst5 = load_list("lst5", offs5)
        lst2 = load_list("lst2", offs2)
        xo_s = tenant("xo_s", [P, M], U8, 1024)
        zero_bytes(nc.gpsimd, xo_s)
        load_scale_rows(xo_s, xo_scales)
        w2_rows = tenant("w2_rows", [P, R], U8, 256)
        zero_bytes(nc.gpsimd, w2_rows)
        load_scale_rows(w2_rows, w2_scales)
        xo_w = sb("xo_w", [P, M], U32)
        nc.sync.dma_start(xo_w[:].bitcast(I32), xo_words[0].rearrange("p c k -> p (c k)").bitcast(I32))
        w2_raw = sb("w2_raw", [P, 2 * R], U8)
        nc.sync.dma_start(w2_raw[:].bitcast(I32), w2_words[0].bitcast(I32))
        lst6 = load_list("lst6", offs6)
        vs_s = sb("vs_s", [P, V], U8, tag="shared")
        zero_bytes(nc.gpsimd, vs_s)
        load_scale_rows(vs_s, vs_scales)
        vs_w = sb("vs_w", [P, V], U16)
        nc.sync.dma_start(vs_w[:].bitcast(I32), vs_words[0].bitcast(I32))


        w2_w = sb("w2_w", [P, PACK, P, 2], U8)
        nc.vector.tensor_copy(w2_w[:], w2_raw[:].rearrange("p (m t b) -> p t m b", t=PACK, b=2))
        w2_s = sb("w2_s", [P, PACK, P], U8)
        nc.vector.tensor_copy(w2_s[:], w2_rows[:].rearrange("p (m t) -> p t m", t=PACK))
        xo_gw = sb("xo_gw", [P, J], U32)
        xo_gs = sb("xo_gs", [P, J], U8)
        nc.vector.tensor_copy(xo_gw[:], xo_w[:].indirect(lst2[:]))
        nc.vector.tensor_copy(xo_gs[:], xo_s[:].indirect(lst2[:]))
        b_ps = []
        for t in range(PACK):
            ps = bank("b_ps%d" % t, J)
            nc.tensor.matmul_mx(
                ps[:], lhsT=w2_w[:, t, :, :].rearrange("p m b -> p (m b)").bitcast(FP4X4), lhsT_scale=w2_s[:, t, :],
                rhs=xo_gw[:].bitcast(FP8X4), rhs_scale=xo_gs[:], start=True, stop=True,
            )
            b_ps.append(ps)

        vs_gw = sb("vs_gw", [P, N], U16)
        vs_gs = sb("vs_gs", [P, N], U8)
        nc.vector.tensor_copy(vs_gw[:], vs_w[:].indirect(lst6[:]))
        nc.vector.tensor_copy(vs_gs[:], vs_s[:].indirect(lst6[:]))

        groups = ((0, 128), (128, 256), (256, J))
        planes = [sb("planes%d" % g, [P, PACK, hi - lo], BF16) for g, (lo, hi) in enumerate(groups)]
        hid = [sb("hid%d" % c, [P, 128, PACK], BF16) for c in range(4)]
        returns = [sb("returns%d" % t, [P, S], F32) for t in range(PACK)]

        def fetch(t):
            nc.scalar.activation(returns[t][:], boards[t % 2][:].indirect(lst4[:]), COPY, scale=sa_sb[:, t : t + 1])

        def put_back(t):
            scatter(slots[t % 2], lst5[:], returns[t][:])

        def larger(t, g):
            lo, hi = groups[g]
            nc.vector.tensor_tensor(planes[g][:, t, :], slots[t % 2][:, lo:hi], b_ps[t][:, lo:hi], MAX)

        def weave(copy, t, c):
            g = min(c, 2)
            lo = 128 * c - groups[g][0]
            copy(hid[c][:, :, t : t + 2], planes[g][:, t : t + 2, lo : lo + 128].rearrange("p t j -> p j t"))

        for i in (1, 2):
            for t in range(2):
                scatter(boards[t], entries(lst3, pieces[i][0], pieces[i][1]), a_later[i][:, t, :])
        slots = [tenant("slots%d" % i, [P, J], F32, 2048 + 2048 * i) for i in range(2)]
        for tile in slots:
            nc.gpsimd.memset(tile[:], 0.0)
        for t in range(2):
            fetch(t)
        for t in range(2):
            put_back(t)
            for g in range(3):
                larger(t, g)
        for t in range(2):
            scatter(boards[t], lst3[:], a_pair[:, t, :])
        for c in range(4):
            weave(nc.vector.tensor_copy, 0, c)
        for t in range(2, PACK):
            fetch(t)
        put_back(2)
        for g in range(3):
            larger(2, g)
        put_back(3)

        codes = [sb("codes%d" % c, [P, 128], U32) for c in range(4)]
        scales = [sb("scales%d" % c, [P, 128], U8) for c in range(4)]

        def quantise(c):
            nc.vector.quantize_mx(
                out=codes[c][:].bitcast(FP8X4), scales=scales[c][:], in_=hid[c][:].rearrange("p j t -> p (j t)")
            )

        def product_y(dst, u, c):
            rows = slice(u * P, (u + 1) * P)
            nc.tensor.matmul_mx(
                dst, lhsT=vs_gw[:, rows].bitcast(FP4X4), lhsT_scale=vs_gs[:, rows],
                rhs=codes[c][:].bitcast(FP8X4), rhs_scale=scales[c][:], start=True, stop=True,
            )

        def finish(c, copy):
            ps = bank("y_ps%d" % c, 256)
            for u in range(2):
                product_y(ps[:, u * 128 : (u + 1) * 128], u, c)
            y = sb("y%d" % c, [P, 2, 128], F32)
            copy(y[:].rearrange("p u j -> p (u j)"), ps[:])
            nc.sync.dma_start(out[:, 128 * c : 128 * (c + 1)].rearrange("(u p) j -> p u j", u=2), y[:])

        larger(3, 0)
        larger(3, 2)
        weave(nc.scalar.copy, 2, 2)
        weave(nc.scalar.copy, 2, 3)
        weave(nc.vector.tensor_copy, 2, 0)
        larger(3, 1)
        quantise(0)
        weave(nc.vector.tensor_copy, 2, 1)
        quantise(2)
        quantise(1)
        quantise(3)
        finish(0, nc.scalar.copy)
        finish(2, nc.scalar.copy)
        finish(1, nc.vector.tensor_copy)
        for u, copy, queue in ((0, nc.scalar.copy, nc.scalar), (1, nc.vector.tensor_copy, nc.sync)):
            ps = bank("y_ps3%d" % u, 128)
            product_y(ps[:], u, 3)
            y = sb("y3%d" % u, [P, 128], F32)
            copy(y[:], ps[:])
            queue.dma_start(out[u * P : (u + 1) * P, 384:512], y[:])
